import numpy as np
import ml_dtypes


def mxq(x, axis, fmt="e4m3"):
    dtype, down = {"e4m3": (ml_dtypes.float8_e4m3fn, 7), "e5m2": (ml_dtypes.float8_e5m2, 14)}[fmt]
    v = np.moveaxis(np.asarray(x, np.float32).astype(ml_dtypes.bfloat16).astype(np.float64), axis, -1)
    blocks = v.reshape(v.shape[:-1] + (-1, 32))
    amax = np.abs(blocks).max(-1, keepdims=True)
    byte = np.maximum(np.where(amax > 0, np.frexp(amax)[1] - 1 + 127, 0) - down, 1)
    scale = np.exp2(byte - 127.0)
    codes = (blocks / scale).astype(np.float32).astype(dtype).astype(np.float64)
    return np.moveaxis((codes * scale).reshape(v.shape), -1, axis)


WIDE = False


def mx_kscale(k):
    if not WIDE:
        return np.ones(k)
    levels = np.array([10, -10, 5, -5, 0])
    if k % 512:
        return np.exp2(np.random.permutation(np.resize(levels, k // 32))).repeat(32)
    a = np.empty((k // 512, 16))
    for p in range(k // 512):
        a[p, :8] = np.random.permutation(np.resize(levels, 8))
        for g in range(8):
            far = levels[np.abs(levels - a[p, g]) >= 10]
            a[p, g + 8] = far[np.random.randint(len(far))]
    return np.exp2(a.ravel()).repeat(32)


def f64(x):
    return np.asarray(x).astype(np.float64)


def striped(idx):
    return np.tile(idx.reshape(-1, 16).T, (8, 1)).astype(np.uint16)


def unstriped(offs):
    return offs[:16].T.reshape(-1).astype(np.int64)


E2M1 = np.array([0.0, 0.5, 1.0, 1.5, 2.0, 3.0, 4.0, 6.0, -0.0, -0.5, -1.0, -1.5, -2.0, -3.0, -4.0, -6.0])


def pack_weight(w, fmt):
    k, n = w.shape
    w = f64(np.asarray(w, np.float32).astype(ml_dtypes.bfloat16)).reshape(k // 32, 32, n)
    amax = np.abs(w).max(1)
    if fmt == "e4m3":
        byte = np.frexp(amax)[1] - 1 + 127 - 7
    else:
        mant, ex = np.frexp(amax / 6.0)
        byte = np.where(mant > 0.5, ex, ex - 1) + 127
    byte = np.clip(np.where(amax > 0, byte, 1), 1, 254)
    scaled = (w * np.exp2(127.0 - byte)[:, None, :]).reshape(k, n).astype(np.float32)
    by_word = np.ascontiguousarray(scaled.reshape(k // 512, 128, 4, n).transpose(0, 1, 3, 2))
    if fmt == "e4m3":
        words = by_word.astype(ml_dtypes.float8_e4m3fn).view(np.uint8)
    else:
        c = by_word.astype(ml_dtypes.float4_e2m1fn).view(np.uint8) & 0xF
        words = (c[..., 0::2] | (c[..., 1::2] << 4)).reshape(k // 512, 128, 2 * n)
    return np.ascontiguousarray(words), np.ascontiguousarray(byte.astype(np.uint8).reshape(k // 512, 16, n))


def unpack_weight(words, scales, fmt):
    g, _, n = scales.shape
    words = np.ascontiguousarray(words).reshape(g, 128, n, -1)
    if fmt == "e4m3":
        vals = words.view(ml_dtypes.float8_e4m3fn).astype(np.float64)
    else:
        nib = np.empty((g, 128, n, 4), np.uint8)
        nib[..., 0::2] = words & 0xF
        nib[..., 1::2] = words >> 4
        vals = E2M1[nib]
    vals = vals * np.repeat(np.exp2(scales.astype(np.float64) - 127.0), 8, axis=1)[..., None]
    return vals.transpose(0, 1, 3, 2).reshape(g * 512, n)


def gelu(v):
    return 0.5 * v * (1.0 + np.tanh(np.sqrt(2.0 / np.pi) * (v + 0.044715 * v**3)))


K, T, S, H, T2, P, N = 1536, 2048, 1024, 512, 2048, 1024, 512

def setup_inputs():
    n = np.random.standard_normal
    s = mx_kscale(K)[:, None]
    u = mx_kscale(H)[:, None]
    tab_words, tab_scales = pack_weight(n((K, T)) * s, "e4m3")
    w1_words, w1_scales = pack_weight(1.5 * n((K, H)) / np.sqrt(K) / s, "e2m1")
    return {
        "tab_words": tab_words, "tab_scales": tab_scales,
        "offs": striped(np.random.permutation(T)[:S]),
        "w1_words": w1_words, "w1_scales": w1_scales,
        "w2": (1.4 * n((K, H)) / np.sqrt(K) / s).astype(np.float32),
        "gain": (np.exp(0.3 * n(H)) * u[:, 0]).astype(np.float32),
        "wgs": np.exp(0.3 * n((128, S))).astype(np.float32),
        "page0": (n((H, T2)) * u).astype(np.float32),
        "offs2": striped(np.random.permutation(T2)[:S]),
        "offs3": striped(np.random.permutation(T2)[:P]),
        "offs4": striped(np.random.permutation(T2)[:P]),
        "gm": np.exp(0.4 * n((H, P))).astype(np.float32),
        "w4": (n((H, N)) / np.sqrt(H) / u).astype(np.float32),
    }

def reference(tab_words, tab_scales, offs, w1_words, w1_scales, w2, gain, wgs, page0, offs2, offs3, offs4, gm, w4):
    v = unpack_weight(tab_words, tab_scales, "e4m3")[:, unstriped(offs)]
    w1 = unpack_weight(w1_words, w1_scales, "e2m1")
    w2q = mxq(f64(w2), 0, "e4m3")
    d = w1.T @ v
    f = w2q.T @ v
    h = np.abs(d) * np.tanh(f) * f64(gain)[:, None]
    before = f64(page0)
    page = before.copy()
    page[:, unstriped(offs2)] = np.tile(f64(wgs), (H // 128, 1)) * h
    x = (page[:, unstriped(offs3)] + before[:, unstriped(offs4)]) * f64(gm)
    xq = mxq(x, 0, "e4m3")
    w4q = mxq(f64(w4), 0, "e4m3")
    out = w4q.T @ xq
    return out

@@ -1,0 +1,270 @@
+from contextlib import ExitStack
+
+import concourse.mybir as mybir
+from concourse.masks import make_identity
+
+K, T, S, H, T2, M_OUT, N_OUT = 1536, 2048, 1024, 512, 2048, 1024, 512
+FLOPS = 2 * K * H * S * 2 + 2 * H * N_OUT * M_OUT
+
+F32 = mybir.dt.float32
+BF16 = mybir.dt.bfloat16
+I32 = mybir.dt.int32
+U32 = mybir.dt.uint32
+U16 = mybir.dt.uint16
+U8 = mybir.dt.uint8
+FP8X4 = mybir.dt.float8_e4m3fn_x4
+FP4X4 = mybir.dt.float4_e2m1fn_x4
+MULT = mybir.AluOpType.mult
+ACT = mybir.ActivationFunctionType
+
+P = 128
+PACK = 4
+PASSES = K // (P * PACK)
+ROW_TILES = H // P
+HALF = 512
+HALVES = S // HALF
+LIST_COLS = S // 16
+SHIFT_ROWS = 112
+CHUNKS = (256, 256, 256, 128, 128)
+
+
+def tile_list_wall_thinning_scores_kernel(
+    tc, tab_words, tab_scales, offs, w1_words, w1_scales, w2, gain, wgs, page0, offs2, offs3, offs4, gm, w4, out
+):
+    nc = tc.nc
+    with ExitStack() as ctx:
+        keep = ctx.enter_context(tc.tile_pool(name="keep", bufs=1))
+        ring = ctx.enter_context(tc.tile_pool(name="ring", bufs=2))
+        psum = ctx.enter_context(tc.psum_pool(name="psum", bufs=6))
+
+        def bank(shape):
+            return psum.tile(shape, F32, name="bank")
+
+        lists = [keep.tile([P, LIST_COLS], U16, name="list%d" % i) for i in range(4)]
+        table = [keep.tile([P, T], U32, name="table%d" % a) for a in range(PASSES)]
+        table_scales = keep.tile([P, T], U8, name="table_scales")
+        v_codes = [
+            [keep.tile([P, HALF], U32, name="v_codes%d_%d" % (a, h), align_bytes=64) for h in range(HALVES)]
+            for a in range(PASSES)
+        ]
+        v_scales = [keep.tile([P, S], U8, name="v_scales0", align_bytes=64)]
+        w1_codes = keep.tile([P, PASSES, 2 * H], U8, name="w1_codes", align_bytes=64)
+        w1_planes = keep.tile([P, PASSES, H], U8, name="w1_planes", align_bytes=64)
+        gain_sb = keep.tile([P, ROW_TILES], F32, name="gain_sb")
+        wgs_sb = [keep.tile([P, HALF], F32, name="wgs_sb%d" % h) for h in range(HALVES)]
+        page = [keep.tile([P, T2], F32, name="page%d" % t) for t in range(ROW_TILES)]
+        before = [keep.tile([P, T2], F32, name="before%d" % t) for t in range(ROW_TILES)]
+        gm_sb = [keep.tile([P, ROW_TILES, w], F32, name="gm_sb%d" % c) for c, w in enumerate(CHUNKS)]
+        ident = keep.tile([P, P], F32, name="ident")
+
+        nc.gpsimd.memset(table_scales[:].bitcast(I32), 0)
+        nc.vector.memset(w1_planes[:].rearrange("p a c -> p (a c)").bitcast(I32), 0)
+
+        w2_raw = {}
+
+        def load_table(a):
+            nc.sync.dma_start(table[a][:].bitcast(I32), tab_words[a].rearrange("p t i -> p (t i)").bitcast(I32))
+
+        def load_w2(t):
+            for a in range(PASSES):
+                if t == 0:
+                    w2_raw[t, a] = keep.tile([P, PACK, P], F32, name="w2_first", tag="first%d" % a, align_bytes=64)
+                else:
+                    w2_raw[t, a] = ring.tile([P, PACK, P], F32, name="w2_raw", bufs=2 * PASSES)
+                rows = w2[a * P * PACK : (a + 1) * P * PACK, t * P : (t + 1) * P]
+                nc.sync.dma_start(w2_raw[t, a][:], rows.rearrange("(p i) c -> p i c", i=PACK))
+
+        for i, source in enumerate((offs, offs2, offs3, offs4)):
+            nc.sync.dma_start(lists[i][:], source)
+        load_table(0)
+        for q in range(4):
+            nc.sync.dma_start(
+                table_scales[32 * q : 32 * q + 4 * PASSES, :].bitcast(I32),
+                tab_scales[:, 4 * q : 4 * q + 4, :].bitcast(I32),
+            )
+        make_identity(nc, ident[:])
+        load_w2(0)
+        load_table(1)
+        nc.sync.dma_start(w1_codes[:].bitcast(I32), w1_words.rearrange("a p c -> p a c").bitcast(I32))
+        for q in range(4):
+            nc.sync.dma_start(
+                w1_planes[32 * q : 32 * q + 4, :, :].bitcast(I32),
+                w1_scales[:, 4 * q : 4 * q + 4, :].rearrange("a r c -> r a c").bitcast(I32),
+            )
+        load_table(2)
+        with nc.allow_non_contiguous_dma(reason="one gain value for each partition and row tile"):
+            nc.sync.dma_start(gain_sb[:], gain.rearrange("(t p) -> p t", p=P))
+
+        def gather_words(a):
+            for h in range(HALVES):
+                cols = slice(h * HALF // 16, (h + 1) * HALF // 16)
+                nc.vector.tensor_copy(v_codes[a][h][:], table[a][:].indirect(lists[0][:, cols]))
+
+        w2_codes, w2_planes = {}, {}
+
+        def quantise_w2(t):
+            woven = keep.tile([P, PASSES, P, PACK], BF16, name="w2_woven%d" % t, tag="turn%d" % t, align_bytes=64)
+            for a in range(PASSES):
+                nc.scalar.copy(
+                    woven[:, a].rearrange("p (c j) i -> p c i j", j=4),
+                    w2_raw[t, a][:].rearrange("p i (c j) -> p c i j", j=4),
+                )
+            w2_codes[t] = keep.tile([P, PASSES * P], U32, name="w2_codes%d" % t, align_bytes=64)
+            w2_planes[t] = keep.tile([P, PASSES * P], U8, name="w2_planes%d" % t, align_bytes=64)
+            nc.vector.quantize_mx(
+                w2_codes[t][:].bitcast(FP8X4), w2_planes[t][:], woven[:].rearrange("p a c i -> p (a c i)")
+            )
+
+        gather_words(0)
+        nc.vector.tensor_copy(v_scales[0][:], table_scales[:].indirect(lists[0][:]))
+        quantise_w2(0)
+        for a in range(1, PASSES):
+            v_scales.append(keep.tile([P, S], U8, name="v_scales", tag="first%d" % a, align_bytes=64))
+            nc.gpsimd.memset(v_scales[a][:].bitcast(I32), 0)
+            nc.sync.dma_start(
+                v_scales[a][:SHIFT_ROWS, :].bitcast(I32), v_scales[0][4 * a : 4 * a + SHIFT_ROWS, :].bitcast(I32)
+            )
+        nc.sync.dma_start(wgs_sb[0][:], wgs[:, :HALF])
+        nc.sync.dma_start(page[0][:], page0[:P, :])
+        load_w2(1)
+        nc.sync.dma_start(wgs_sb[1][:], wgs[:, HALF:])
+
+        gather_words(1)
+        gather_words(2)
+
+        def make_h(t, h):
+            cols = slice(h * HALF, (h + 1) * HALF)
+            f_ps = bank([P, HALF])
+            d_ps = bank([P, HALF])
+            for a in range(PASSES):
+                nc.tensor.matmul_mx(
+                    f_ps[:],
+                    lhsT=w2_codes[t][:, a * P : (a + 1) * P].bitcast(FP8X4),
+                    lhsT_scale=w2_planes[t][:, a * P : (a + 1) * P],
+                    rhs=v_codes[a][h][:].bitcast(FP8X4),
+                    rhs_scale=v_scales[a][:, cols],
+                    start=(a == 0),
+                    stop=(a == PASSES - 1),
+                )
+                nc.tensor.matmul_mx(
+                    d_ps[:],
+                    lhsT=w1_codes[:, a, 2 * t * P : 2 * (t + 1) * P].bitcast(FP4X4),
+                    lhsT_scale=w1_planes[:, a, t * P : (t + 1) * P],
+                    rhs=v_codes[a][h][:].bitcast(FP8X4),
+                    rhs_scale=v_scales[a][:, cols],
+                    start=(a == 0),
+                    stop=(a == PASSES - 1),
+                )
+            tanh_f = ring.tile([P, HALF], F32, name="tanh_f", bufs=3)
+            abs_d = ring.tile([P, HALF], F32, name="abs_d", bufs=3)
+            nc.scalar.activation(tanh_f[:], f_ps[:], ACT.Tanh)
+            nc.scalar.activation(abs_d[:], d_ps[:], ACT.Abs)
+            unit = HALVES * t + h
+            if 1 <= unit < ROW_TILES:
+                h_sb = keep.tile([P, HALF], F32, name="h_held%d" % unit, tag="turn%d" % unit, align_bytes=64)
+            else:
+                h_sb = ring.tile([P, HALF], F32, name="h_sb")
+            nc.vector.scalar_tensor_tensor(h_sb[:], abs_d[:], gain_sb[:, t : t + 1], tanh_f[:], MULT, MULT)
+            return h_sb
+
+        def put(t, h, h_sb):
+            cols = slice(h * HALF // 16, (h + 1) * HALF // 16)
+            nc.vector.tensor_tensor(page[t][:].indirect(lists[1][:, cols]), h_sb[:], wgs_sb[h][:], MULT)
+
+        for t in range(1, ROW_TILES):
+            if t + 1 < ROW_TILES:
+                load_w2(t + 1)
+            nc.sync.dma_start(page[t][:], page0[t * P : (t + 1) * P, :])
+        starts = [sum(CHUNKS[:c]) for c in range(len(CHUNKS))]
+        gm_rows = gm.rearrange("(t p) m -> p t m", p=P)
+        nc.sync.dma_start(gm_sb[0][:], gm_rows[:, :, : CHUNKS[0]])
+        for t in range(ROW_TILES):
+            nc.sync.dma_start(before[t][:], page0[t * P : (t + 1) * P, :])
+        w4_raw = keep.tile([P, PACK, N_OUT], F32, name="w4_raw")
+        nc.sync.dma_start(w4_raw[:], w4.rearrange("(p i) n -> p i n", i=PACK))
+        for c in range(1, len(CHUNKS)):
+            nc.sync.dma_start(gm_sb[c][:], gm_rows[:, :, starts[c] : starts[c] + CHUNKS[c]])
+
+        units = [(t, h) for t in range(ROW_TILES) for h in range(HALVES)]
+        made = make_h(*units[0])
+        for u, (t, h) in enumerate(units):
+            if u + 1 < ROW_TILES:
+                quantise_w2(u + 1)
+            following = make_h(*units[u + 1]) if u + 1 < len(units) else None
+            put(t, h, made)
+            made = following
+
+        w4_woven = keep.tile([P, N_OUT, PACK], BF16, name="w4_woven", align_bytes=64)
+        nc.scalar.copy(
+            w4_woven[:].rearrange("p (c j) i -> p c i j", j=4), w4_raw[:].rearrange("p i (c j) -> p c i j", j=4)
+        )
+        w4_codes = keep.tile([P, N_OUT], U32, name="w4_codes", align_bytes=64)
+        w4_plane = keep.tile([P, N_OUT], U8, name="w4_plane", align_bytes=64)
+
+        def quantise_x(c, woven):
+            x_codes = ring.tile([P, CHUNKS[c]], U32, name="x_codes", align_bytes=64)
+            x_plane = ring.tile([P, CHUNKS[c]], U8, name="x_plane", align_bytes=64)
+            nc.vector.quantize_mx(x_codes[:].bitcast(FP8X4), x_plane[:], woven[:])
+            return x_codes, x_plane
+
+        def fetch(c):
+            width = CHUNKS[c]
+            cols = slice(starts[c] // 16, (starts[c] + width) // 16)
+            blocks = width // P
+            sums = [psum.tile([P, H], F32, name="sums", bufs=2) for b in range(blocks)]
+            for t in range(ROW_TILES):
+                old = ring.tile([P, width], F32, name="old", bufs=ROW_TILES)
+                nc.vector.tensor_tensor(old[:], before[t][:].indirect(lists[3][:, cols]), gm_sb[c][:, t, :], MULT)
+                new = ring.tile([P, width], F32, name="new", bufs=ROW_TILES)
+                nc.vector.tensor_tensor(new[:], page[t][:].indirect(lists[2][:, cols]), gm_sb[c][:, t, :], MULT)
+                for b in range(blocks):
+                    target = sums[b][:, t * P : (t + 1) * P]
+                    block = slice(b * P, (b + 1) * P)
+                    nc.tensor.matmul(target, old[:, block], ident[:], start=True, stop=False, is_transpose=True)
+                    nc.tensor.matmul(target, new[:, block], ident[:], start=False, stop=True, is_transpose=True)
+            back = bank([P, blocks, 2, P])
+            for b in range(blocks):
+                x_t = ring.tile([P, H], BF16, name="x_t", bufs=3)
+                nc.scalar.copy(
+                    x_t[:].rearrange("m (u p e) -> m u p e", u=2, e=2),
+                    sums[b][:].rearrange("m (p u e) -> m u p e", u=2, e=2),
+                )
+                for u in range(2):
+                    nc.tensor.transpose(back[:, b, u, :], x_t[:].bitcast(F32)[:, u * P : (u + 1) * P], ident[:])
+            woven = ring.tile([P, width * PACK], BF16, name="x_woven", align_bytes=64)
+            nc.scalar.copy(
+                woven[:].bitcast(F32).rearrange("p (b m u) -> p b m u", b=blocks, u=2),
+                back[:].rearrange("p b u m -> p b m u"),
+            )
+            return woven
+
+        out_rows = out.rearrange("(j p) m -> p j m", p=P)
+
+        def score(c, x_codes, x_plane):
+            width = CHUNKS[c]
+            for pair in range(2):
+                acc = bank([P, 2, width])
+                for j in range(2):
+                    n_cols = slice((2 * pair + j) * P, (2 * pair + j + 1) * P)
+                    nc.tensor.matmul_mx(
+                        acc[:, j, :],
+                        lhsT=w4_codes[:, n_cols].bitcast(FP8X4),
+                        lhsT_scale=w4_plane[:, n_cols],
+                        rhs=x_codes[:].bitcast(FP8X4),
+                        rhs_scale=x_plane[:],
+                        start=True,
+                        stop=True,
+                    )
+                staged = ring.tile([P, 2, width], F32, name="staged", bufs=5)
+                if 2 * len(CHUNKS) - 4 <= 2 * c + pair < 2 * len(CHUNKS) - 1:
+                    nc.vector.tensor_copy(staged[:], acc[:])
+                else:
+                    nc.scalar.copy(staged[:], acc[:])
+                nc.sync.dma_start(out_rows[:, 2 * pair : 2 * pair + 2, starts[c] : starts[c] + width], staged[:])
+
+        nc.vector.quantize_mx(w4_codes[:].bitcast(FP8X4), w4_plane[:], w4_woven[:].rearrange("p n i -> p (n i)"))
+        waiting = fetch(0)
+        for c in range(len(CHUNKS)):
+            following = fetch(c + 1) if c + 1 < len(CHUNKS) else None
+            score(c, *quantise_x(c, waiting))
+            waiting = following

@@ -25,7 +25,11 @@ HALF = 512
 HALVES = S // HALF
 LIST_COLS = S // 16
 SHIFT_ROWS = 112
+WHOLE = ((0, S),)
+IN_HALVES = ((0, HALF), (HALF, HALF))
+FIRST_PIECES = ((0, HALF // 2), (HALF // 2, HALF // 2), (HALF, HALF))
 CHUNKS = (256, 256, 256, 128, 128)
+LAST = len(CHUNKS) - 1
 
 
 def tile_list_wall_thinning_scores_kernel(
@@ -43,12 +47,11 @@ def tile_list_wall_thinning_scores_kernel(
         lists = [keep.tile([P, LIST_COLS], U16, name="list%d" % i) for i in range(4)]
         table = [keep.tile([P, T], U32, name="table%d" % a) for a in range(PASSES)]
         table_scales = keep.tile([P, T], U8, name="table_scales")
-        v_codes = [
-            [keep.tile([P, HALF], U32, name="v_codes%d_%d" % (a, h), align_bytes=64) for h in range(HALVES)]
-            for a in range(PASSES)
-        ]
+        v_codes = {a: keep.tile([P, S], U32, name="v_codes%d" % a, align_bytes=64) for a in range(PASSES)}
         v_scales = [keep.tile([P, S], U8, name="v_scales0", align_bytes=64)]
-        w1_codes = keep.tile([P, PASSES, 2 * H], U8, name="w1_codes", align_bytes=64)
+        w1_first = keep.tile([P, PASSES, 2 * P], U8, name="w1_first", align_bytes=64)
+        w1_rest = keep.tile([P, PASSES, 2 * (H - P)], U8, name="w1_rest", align_bytes=64)
+        w1_rows = w1_words.rearrange("a p c -> p a c")
         w1_planes = keep.tile([P, PASSES, H], U8, name="w1_planes", align_bytes=64)
         gain_sb = keep.tile([P, ROW_TILES], F32, name="gain_sb")
         wgs_sb = [keep.tile([P, HALF], F32, name="wgs_sb%d" % h) for h in range(HALVES)]
@@ -74,6 +77,8 @@ def tile_list_wall_thinning_scores_kernel(
                 rows = w2[a * P * PACK : (a + 1) * P * PACK, t * P : (t + 1) * P]
                 nc.sync.dma_start(w2_raw[t, a][:], rows.rearrange("(p i) c -> p i c", i=PACK))
 
+        with nc.allow_non_contiguous_dma(reason="one gain value for each partition and row tile"):
+            nc.gpsimd.dma_start(gain_sb[:], gain.rearrange("(t p) -> p t", p=P))
         for i, source in enumerate((offs, offs2, offs3, offs4)):
             nc.sync.dma_start(lists[i][:], source)
         load_table(0)
@@ -85,25 +90,28 @@ def tile_list_wall_thinning_scores_kernel(
         make_identity(nc, ident[:])
         load_w2(0)
         load_table(1)
-        nc.sync.dma_start(w1_codes[:].bitcast(I32), w1_words.rearrange("a p c -> p a c").bitcast(I32))
+        nc.sync.dma_start(w1_first[:].bitcast(I32), w1_rows[:, :, : 2 * P].bitcast(I32))
         for q in range(4):
             nc.sync.dma_start(
                 w1_planes[32 * q : 32 * q + 4, :, :].bitcast(I32),
                 w1_scales[:, 4 * q : 4 * q + 4, :].rearrange("a r c -> r a c").bitcast(I32),
             )
         load_table(2)
-        with nc.allow_non_contiguous_dma(reason="one gain value for each partition and row tile"):
-            nc.sync.dma_start(gain_sb[:], gain.rearrange("(t p) -> p t", p=P))
 
-        def gather_words(a):
-            for h in range(HALVES):
-                cols = slice(h * HALF // 16, (h + 1) * HALF // 16)
-                nc.vector.tensor_copy(v_codes[a][h][:], table[a][:].indirect(lists[0][:, cols]))
+        gain_sign = keep.tile([P, ROW_TILES], F32, name="gain_sign")
+        nc.scalar.activation(gain_sign[:], gain_sb[:], ACT.Sign)
+
+        def gather_words(a, pieces):
+            for first, width in pieces:
+                nc.vector.tensor_copy(
+                    v_codes[a][:, first : first + width],
+                    table[a][:].indirect(lists[0][:, first // 16 : (first + width) // 16]),
+                )
 
         w2_codes, w2_planes = {}, {}
 
         def quantise_w2(t):
-            woven = keep.tile([P, PASSES, P, PACK], BF16, name="w2_woven%d" % t, tag="turn%d" % t, align_bytes=64)
+            woven = ring.tile([P, PASSES, P, PACK], BF16, name="w2_woven", align_bytes=64)
             for a in range(PASSES):
                 nc.scalar.copy(
                     woven[:, a].rearrange("p (c j) i -> p c i j", j=4),
@@ -115,7 +123,7 @@ def tile_list_wall_thinning_scores_kernel(
                 w2_codes[t][:].bitcast(FP8X4), w2_planes[t][:], woven[:].rearrange("p a c i -> p (a c i)")
             )
 
-        gather_words(0)
+        gather_words(0, WHOLE)
         nc.vector.tensor_copy(v_scales[0][:], table_scales[:].indirect(lists[0][:]))
         quantise_w2(0)
         for a in range(1, PASSES):
@@ -127,49 +135,55 @@ def tile_list_wall_thinning_scores_kernel(
         nc.sync.dma_start(wgs_sb[0][:], wgs[:, :HALF])
         nc.sync.dma_start(page[0][:], page0[:P, :])
         load_w2(1)
+        nc.sync.dma_start(w1_rest[:].bitcast(I32), w1_rows[:, :, 2 * P :].bitcast(I32))
         nc.sync.dma_start(wgs_sb[1][:], wgs[:, HALF:])
 
-        gather_words(1)
-        gather_words(2)
+        gather_words(1, WHOLE)
+        gather_words(2, FIRST_PIECES)
 
-        def make_h(t, h):
-            cols = slice(h * HALF, (h + 1) * HALF)
-            f_ps = bank([P, HALF])
-            d_ps = bank([P, HALF])
+        units = [(t, first, width) for t in range(ROW_TILES) for first, width in (IN_HALVES if t > 1 else FIRST_PIECES)]
+
+        def make_h(unit):
+            t, first, width = units[unit]
+            cols = slice(first, first + width)
+            w1_codes, w1_t = (w1_first, 0) if t == 0 else (w1_rest, t - 1)
+            f_ps = bank([P, width])
+            d_ps = bank([P, width])
             for a in range(PASSES):
                 nc.tensor.matmul_mx(
                     f_ps[:],
                     lhsT=w2_codes[t][:, a * P : (a + 1) * P].bitcast(FP8X4),
                     lhsT_scale=w2_planes[t][:, a * P : (a + 1) * P],
-                    rhs=v_codes[a][h][:].bitcast(FP8X4),
+                    rhs=v_codes[a][:, cols].bitcast(FP8X4),
                     rhs_scale=v_scales[a][:, cols],
                     start=(a == 0),
                     stop=(a == PASSES - 1),
                 )
                 nc.tensor.matmul_mx(
                     d_ps[:],
-                    lhsT=w1_codes[:, a, 2 * t * P : 2 * (t + 1) * P].bitcast(FP4X4),
+                    lhsT=w1_codes[:, a, 2 * w1_t * P : 2 * (w1_t + 1) * P].bitcast(FP4X4),
                     lhsT_scale=w1_planes[:, a, t * P : (t + 1) * P],
-                    rhs=v_codes[a][h][:].bitcast(FP8X4),
+                    rhs=v_codes[a][:, cols].bitcast(FP8X4),
                     rhs_scale=v_scales[a][:, cols],
                     start=(a == 0),
                     stop=(a == PASSES - 1),
                 )
-            tanh_f = ring.tile([P, HALF], F32, name="tanh_f", bufs=3)
-            abs_d = ring.tile([P, HALF], F32, name="abs_d", bufs=3)
-            nc.scalar.activation(tanh_f[:], f_ps[:], ACT.Tanh)
-            nc.scalar.activation(abs_d[:], d_ps[:], ACT.Abs)
-            unit = HALVES * t + h
-            if 1 <= unit < ROW_TILES:
-                h_sb = keep.tile([P, HALF], F32, name="h_held%d" % unit, tag="turn%d" % unit, align_bytes=64)
-            else:
-                h_sb = ring.tile([P, HALF], F32, name="h_sb")
-            nc.vector.scalar_tensor_tensor(h_sb[:], abs_d[:], gain_sb[:, t : t + 1], tanh_f[:], MULT, MULT)
-            return h_sb
+            tanh_f = ring.tile([P, width], F32, name="tanh_f", bufs=3)
+            abs_d = ring.tile([P, width], F32, name="abs_d", bufs=3)
+            nc.scalar.activation(tanh_f[:], f_ps[:], ACT.Tanh, scale=gain_sign[:, t : t + 1])
+            nc.scalar.activation(abs_d[:], d_ps[:], ACT.Abs, scale=gain_sb[:, t : t + 1])
+            engine = nc.vector if unit < 2 else nc.gpsimd
+            h_sb = ring.tile([P, width], F32, name="h_sb")
+            engine.tensor_tensor(h_sb[:], abs_d[:], tanh_f[:], MULT)
+            h, inside = divmod(first, HALF)
+            weighted = ring.tile([P, width], F32, name="weighted", bufs=3)
+            engine.tensor_tensor(weighted[:], h_sb[:], wgs_sb[h][:, inside : inside + width], MULT)
+            return weighted
 
-        def put(t, h, h_sb):
-            cols = slice(h * HALF // 16, (h + 1) * HALF // 16)
-            nc.vector.tensor_tensor(page[t][:].indirect(lists[1][:, cols]), h_sb[:], wgs_sb[h][:], MULT)
+        def put(unit, weighted):
+            t, first, width = units[unit]
+            places = lists[1][:, first // 16 : (first + width) // 16]
+            nc.vector.tensor_copy(page[t][:].indirect(places), weighted[:])
 
         for t in range(1, ROW_TILES):
             if t + 1 < ROW_TILES:
@@ -185,13 +199,12 @@ def tile_list_wall_thinning_scores_kernel(
         for c in range(1, len(CHUNKS)):
             nc.sync.dma_start(gm_sb[c][:], gm_rows[:, :, starts[c] : starts[c] + CHUNKS[c]])
 
-        units = [(t, h) for t in range(ROW_TILES) for h in range(HALVES)]
-        made = make_h(*units[0])
-        for u, (t, h) in enumerate(units):
-            if u + 1 < ROW_TILES:
-                quantise_w2(u + 1)
-            following = make_h(*units[u + 1]) if u + 1 < len(units) else None
-            put(t, h, made)
+        made = make_h(0)
+        for u in range(len(units)):
+            if u % 2 == 1 and u // 2 + 1 < ROW_TILES:
+                quantise_w2(u // 2 + 1)
+            following = make_h(u + 1) if u + 1 < len(units) else None
+            put(u, made)
             made = following
 
         w4_woven = keep.tile([P, N_OUT, PACK], BF16, name="w4_woven", align_bytes=64)
@@ -256,7 +269,7 @@ def tile_list_wall_thinning_scores_kernel(
                         stop=True,
                     )
                 staged = ring.tile([P, 2, width], F32, name="staged", bufs=5)
-                if 2 * len(CHUNKS) - 4 <= 2 * c + pair < 2 * len(CHUNKS) - 1:
+                if 2 * LAST - 2 <= 2 * c + pair <= 2 * LAST:
                     nc.vector.tensor_copy(staged[:], acc[:])
                 else:
                     nc.scalar.copy(staged[:], acc[:])

@@ -39,13 +39,13 @@ def tile_list_wall_thinning_scores_kernel(
     with ExitStack() as ctx:
         keep = ctx.enter_context(tc.tile_pool(name="keep", bufs=1))
         ring = ctx.enter_context(tc.tile_pool(name="ring", bufs=2))
-        psum = ctx.enter_context(tc.psum_pool(name="psum", bufs=6))
+        psum = ctx.enter_context(tc.psum_pool(name="psum", bufs=4))
 
         def bank(shape):
             return psum.tile(shape, F32, name="bank")
 
         lists = [keep.tile([P, LIST_COLS], U16, name="list%d" % i) for i in range(4)]
-        table = [keep.tile([P, T], U32, name="table%d" % a) for a in range(PASSES)]
+        table = [keep.tile([P, T], U32, name="table%d" % a, tag="table%d" % a) for a in range(PASSES)]
         table_scales = keep.tile([P, T], U8, name="table_scales")
         v_codes = {a: keep.tile([P, S], U32, name="v_codes%d" % a, align_bytes=64) for a in range(PASSES)}
         v_scales = [keep.tile([P, S], U8, name="v_scales0", align_bytes=64)]
@@ -54,7 +54,7 @@ def tile_list_wall_thinning_scores_kernel(
         w1_rows = w1_words.rearrange("a p c -> p a c")
         w1_planes = keep.tile([P, PASSES, H], U8, name="w1_planes", align_bytes=64)
         gain_sb = keep.tile([P, ROW_TILES], F32, name="gain_sb")
-        wgs_sb = [keep.tile([P, HALF], F32, name="wgs_sb%d" % h) for h in range(HALVES)]
+        wgs_sb = keep.tile([P, S], F32, name="wgs_sb")
         page = [keep.tile([P, T2], F32, name="page%d" % t) for t in range(ROW_TILES)]
         before = [keep.tile([P, T2], F32, name="before%d" % t) for t in range(ROW_TILES)]
         gm_sb = [keep.tile([P, ROW_TILES, w], F32, name="gm_sb%d" % c) for c, w in enumerate(CHUNKS)]
@@ -79,16 +79,15 @@ def tile_list_wall_thinning_scores_kernel(
 
         with nc.allow_non_contiguous_dma(reason="one gain value for each partition and row tile"):
             nc.gpsimd.dma_start(gain_sb[:], gain.rearrange("(t p) -> p t", p=P))
-        for i, source in enumerate((offs, offs2, offs3, offs4)):
-            nc.sync.dma_start(lists[i][:], source)
+        nc.sync.dma_start(lists[0][:], offs)
         load_table(0)
+        load_w2(0)
         for q in range(4):
             nc.sync.dma_start(
                 table_scales[32 * q : 32 * q + 4 * PASSES, :].bitcast(I32),
                 tab_scales[:, 4 * q : 4 * q + 4, :].bitcast(I32),
             )
         make_identity(nc, ident[:])
-        load_w2(0)
         load_table(1)
         nc.sync.dma_start(w1_first[:].bitcast(I32), w1_rows[:, :, : 2 * P].bitcast(I32))
         for q in range(4):
@@ -97,9 +96,7 @@ def tile_list_wall_thinning_scores_kernel(
                 w1_scales[:, 4 * q : 4 * q + 4, :].rearrange("a r c -> r a c").bitcast(I32),
             )
         load_table(2)
-
-        gain_sign = keep.tile([P, ROW_TILES], F32, name="gain_sign")
-        nc.scalar.activation(gain_sign[:], gain_sb[:], ACT.Sign)
+        nc.sync.dma_start(lists[1][:], offs2)
 
         def gather_words(a, pieces):
             for first, width in pieces:
@@ -111,7 +108,7 @@ def tile_list_wall_thinning_scores_kernel(
         w2_codes, w2_planes = {}, {}
 
         def quantise_w2(t):
-            woven = ring.tile([P, PASSES, P, PACK], BF16, name="w2_woven", align_bytes=64)
+            woven = keep.tile([P, PASSES, P, PACK], BF16, name="w2_woven%d" % t, tag="turn%d" % t, align_bytes=64)
             for a in range(PASSES):
                 nc.scalar.copy(
                     woven[:, a].rearrange("p (c j) i -> p c i j", j=4),
@@ -132,77 +129,81 @@ def tile_list_wall_thinning_scores_kernel(
             nc.sync.dma_start(
                 v_scales[a][:SHIFT_ROWS, :].bitcast(I32), v_scales[0][4 * a : 4 * a + SHIFT_ROWS, :].bitcast(I32)
             )
-        nc.sync.dma_start(wgs_sb[0][:], wgs[:, :HALF])
+        nc.sync.dma_start(wgs_sb[:, :HALF], wgs[:, :HALF])
         nc.sync.dma_start(page[0][:], page0[:P, :])
         load_w2(1)
         nc.sync.dma_start(w1_rest[:].bitcast(I32), w1_rows[:, :, 2 * P :].bitcast(I32))
-        nc.sync.dma_start(wgs_sb[1][:], wgs[:, HALF:])
+        nc.sync.dma_start(wgs_sb[:, HALF:], wgs[:, HALF:])
 
         gather_words(1, WHOLE)
         gather_words(2, FIRST_PIECES)
 
-        units = [(t, first, width) for t in range(ROW_TILES) for first, width in (IN_HALVES if t > 1 else FIRST_PIECES)]
+        pieces = (FIRST_PIECES, IN_HALVES, WHOLE, WHOLE)
+        units = [(t, first, width) for t in range(ROW_TILES) for first, width in pieces[t]]
 
         def make_h(unit):
             t, first, width = units[unit]
-            cols = slice(first, first + width)
             w1_codes, w1_t = (w1_first, 0) if t == 0 else (w1_rest, t - 1)
-            f_ps = bank([P, width])
-            d_ps = bank([P, width])
-            for a in range(PASSES):
-                nc.tensor.matmul_mx(
-                    f_ps[:],
-                    lhsT=w2_codes[t][:, a * P : (a + 1) * P].bitcast(FP8X4),
-                    lhsT_scale=w2_planes[t][:, a * P : (a + 1) * P],
-                    rhs=v_codes[a][:, cols].bitcast(FP8X4),
-                    rhs_scale=v_scales[a][:, cols],
-                    start=(a == 0),
-                    stop=(a == PASSES - 1),
-                )
-                nc.tensor.matmul_mx(
-                    d_ps[:],
-                    lhsT=w1_codes[:, a, 2 * w1_t * P : 2 * (w1_t + 1) * P].bitcast(FP4X4),
-                    lhsT_scale=w1_planes[:, a, t * P : (t + 1) * P],
-                    rhs=v_codes[a][:, cols].bitcast(FP8X4),
-                    rhs_scale=v_scales[a][:, cols],
-                    start=(a == 0),
-                    stop=(a == PASSES - 1),
-                )
-            tanh_f = ring.tile([P, width], F32, name="tanh_f", bufs=3)
-            abs_d = ring.tile([P, width], F32, name="abs_d", bufs=3)
-            nc.scalar.activation(tanh_f[:], f_ps[:], ACT.Tanh, scale=gain_sign[:, t : t + 1])
-            nc.scalar.activation(abs_d[:], d_ps[:], ACT.Abs, scale=gain_sb[:, t : t + 1])
-            engine = nc.vector if unit < 2 else nc.gpsimd
-            h_sb = ring.tile([P, width], F32, name="h_sb")
-            engine.tensor_tensor(h_sb[:], abs_d[:], tanh_f[:], MULT)
-            h, inside = divmod(first, HALF)
-            weighted = ring.tile([P, width], F32, name="weighted", bufs=3)
-            engine.tensor_tensor(weighted[:], h_sb[:], wgs_sb[h][:, inside : inside + width], MULT)
-            return weighted
+            tanh_f = ring.tile([P, width], F32, name="tanh_f")
+            abs_d = ring.tile([P, width], F32, name="abs_d")
+            for inside in range(0, width, HALF):
+                part = slice(inside, min(inside + HALF, width))
+                cols = slice(first + part.start, first + part.stop)
+                f_ps = bank([P, part.stop - part.start])
+                d_ps = bank([P, part.stop - part.start])
+                for a in range(PASSES):
+                    nc.tensor.matmul_mx(
+                        f_ps[:],
+                        lhsT=w2_codes[t][:, a * P : (a + 1) * P].bitcast(FP8X4),
+                        lhsT_scale=w2_planes[t][:, a * P : (a + 1) * P],
+                        rhs=v_codes[a][:, cols].bitcast(FP8X4),
+                        rhs_scale=v_scales[a][:, cols],
+                        start=(a == 0),
+                        stop=(a == PASSES - 1),
+                    )
+                    nc.tensor.matmul_mx(
+                        d_ps[:],
+                        lhsT=w1_codes[:, a, 2 * w1_t * P : 2 * (w1_t + 1) * P].bitcast(FP4X4),
+                        lhsT_scale=w1_planes[:, a, t * P : (t + 1) * P],
+                        rhs=v_codes[a][:, cols].bitcast(FP8X4),
+                        rhs_scale=v_scales[a][:, cols],
+                        start=(a == 0),
+                        stop=(a == PASSES - 1),
+                    )
+                nc.scalar.activation(tanh_f[:, part], f_ps[:], ACT.Tanh)
+                nc.scalar.activation(abs_d[:, part], d_ps[:], ACT.Abs)
+            if 2 <= unit <= ROW_TILES:
+                h_sb = keep.tile([P, width], F32, name="h_held", tag="turn%d" % (unit - 1), align_bytes=64)
+            else:
+                h_sb = ring.tile([P, width], F32, name="h_sb")
+            nc.vector.scalar_tensor_tensor(h_sb[:], abs_d[:], gain_sb[:, t : t + 1], tanh_f[:], MULT, MULT)
+            return h_sb
 
-        def put(unit, weighted):
+        def put(unit, h_sb):
             t, first, width = units[unit]
             places = lists[1][:, first // 16 : (first + width) // 16]
-            nc.vector.tensor_copy(page[t][:].indirect(places), weighted[:])
+            nc.vector.tensor_tensor(page[t][:].indirect(places), h_sb[:], wgs_sb[:, first : first + width], MULT)
 
         for t in range(1, ROW_TILES):
             if t + 1 < ROW_TILES:
                 load_w2(t + 1)
             nc.sync.dma_start(page[t][:], page0[t * P : (t + 1) * P, :])
+        nc.sync.dma_start(lists[2][:], offs3)
+        nc.sync.dma_start(lists[3][:], offs4)
         starts = [sum(CHUNKS[:c]) for c in range(len(CHUNKS))]
         gm_rows = gm.rearrange("(t p) m -> p t m", p=P)
         nc.sync.dma_start(gm_sb[0][:], gm_rows[:, :, : CHUNKS[0]])
         for t in range(ROW_TILES):
             nc.sync.dma_start(before[t][:], page0[t * P : (t + 1) * P, :])
-        w4_raw = keep.tile([P, PACK, N_OUT], F32, name="w4_raw")
+        w4_raw = keep.tile([P, PACK, N_OUT], F32, name="w4_raw", tag="table0")
         nc.sync.dma_start(w4_raw[:], w4.rearrange("(p i) n -> p i n", i=PACK))
         for c in range(1, len(CHUNKS)):
             nc.sync.dma_start(gm_sb[c][:], gm_rows[:, :, starts[c] : starts[c] + CHUNKS[c]])
 
         made = make_h(0)
         for u in range(len(units)):
-            if u % 2 == 1 and u // 2 + 1 < ROW_TILES:
-                quantise_w2(u // 2 + 1)
+            if 1 <= u < ROW_TILES:
+                quantise_w2(u)
             following = make_h(u + 1) if u + 1 < len(units) else None
             put(u, made)
             made = following
@@ -224,27 +225,37 @@ def tile_list_wall_thinning_scores_kernel(
             width = CHUNKS[c]
             cols = slice(starts[c] // 16, (starts[c] + width) // 16)
             blocks = width // P
-            sums = [psum.tile([P, H], F32, name="sums", bufs=2) for b in range(blocks)]
+            sums = [psum.tile([P, H], F32, name="sums") for b in range(blocks)]
+            early = ROW_TILES - 1 if c == LAST else ROW_TILES
+            late = bank([P, H]) if c == LAST else None
             for t in range(ROW_TILES):
-                old = ring.tile([P, width], F32, name="old", bufs=ROW_TILES)
+                old = ring.tile([P, width], F32, name="old", bufs=6)
                 nc.vector.tensor_tensor(old[:], before[t][:].indirect(lists[3][:, cols]), gm_sb[c][:, t, :], MULT)
-                new = ring.tile([P, width], F32, name="new", bufs=ROW_TILES)
+                if c == LAST and t == ROW_TILES - 1:
+                    new = keep.tile([P, width], F32, name="new_held", tag="late", align_bytes=64)
+                else:
+                    new = ring.tile([P, width], F32, name="new", bufs=6)
                 nc.vector.tensor_tensor(new[:], page[t][:].indirect(lists[2][:, cols]), gm_sb[c][:, t, :], MULT)
                 for b in range(blocks):
-                    target = sums[b][:, t * P : (t + 1) * P]
+                    target = (sums[b] if t < early else late)[:, t * P : (t + 1) * P]
                     block = slice(b * P, (b + 1) * P)
                     nc.tensor.matmul(target, old[:, block], ident[:], start=True, stop=False, is_transpose=True)
                     nc.tensor.matmul(target, new[:, block], ident[:], start=False, stop=True, is_transpose=True)
             back = bank([P, blocks, 2, P])
             for b in range(blocks):
                 x_t = ring.tile([P, H], BF16, name="x_t", bufs=3)
-                nc.scalar.copy(
-                    x_t[:].rearrange("m (u p e) -> m u p e", u=2, e=2),
-                    sums[b][:].rearrange("m (p u e) -> m u p e", u=2, e=2),
-                )
+                for source, rows in ((sums[b], slice(0, 32 * early)), (late, slice(32 * early, P))):
+                    if rows.start < rows.stop:
+                        nc.scalar.copy(
+                            x_t[:].rearrange("m (u p e) -> m u p e", u=2, e=2)[:, :, rows, :],
+                            source[:].rearrange("m (p u e) -> m u p e", u=2, e=2)[:, :, rows, :],
+                        )
                 for u in range(2):
                     nc.tensor.transpose(back[:, b, u, :], x_t[:].bitcast(F32)[:, u * P : (u + 1) * P], ident[:])
-            woven = ring.tile([P, width * PACK], BF16, name="x_woven", align_bytes=64)
+            if c == LAST - 2:
+                woven = keep.tile([P, width * PACK], BF16, name="x_woven_late", tag="late", align_bytes=64)
+            else:
+                woven = ring.tile([P, width * PACK], BF16, name="x_woven", align_bytes=64)
             nc.scalar.copy(
                 woven[:].bitcast(F32).rearrange("p (b m u) -> p b m u", b=blocks, u=2),
                 back[:].rearrange("p b u m -> p b m u"),
@@ -273,7 +284,7 @@ def tile_list_wall_thinning_scores_kernel(
                     nc.vector.tensor_copy(staged[:], acc[:])
                 else:
                     nc.scalar.copy(staged[:], acc[:])
-                nc.sync.dma_start(out_rows[:, 2 * pair : 2 * pair + 2, starts[c] : starts[c] + width], staged[:])
+                (nc.scalar if 2 * c + pair == 2 * LAST + 1 else nc.sync).dma_start(out_rows[:, 2 * pair : 2 * pair + 2, starts[c] : starts[c] + width], staged[:])
 
         nc.vector.quantize_mx(w4_codes[:].bitcast(FP8X4), w4_plane[:], w4_woven[:].rearrange("p n i -> p (n i)"))
         waiting = fetch(0)

from contextlib import ExitStack

import concourse.mybir as mybir
from concourse.masks import make_identity

K, T, S, H, T2, M_OUT, N_OUT = 1536, 2048, 1024, 512, 2048, 1024, 512
FLOPS = 2 * K * H * S * 2 + 2 * H * N_OUT * M_OUT

F32 = mybir.dt.float32
BF16 = mybir.dt.bfloat16
I32 = mybir.dt.int32
U32 = mybir.dt.uint32
U16 = mybir.dt.uint16
U8 = mybir.dt.uint8
FP8X4 = mybir.dt.float8_e4m3fn_x4
FP4X4 = mybir.dt.float4_e2m1fn_x4
MULT = mybir.AluOpType.mult
ACT = mybir.ActivationFunctionType

P = 128
PACK = 4
PASSES = K // (P * PACK)
ROW_TILES = H // P
HALF = 512
HALVES = S // HALF
LIST_COLS = S // 16
SHIFT_ROWS = 112
WHOLE = ((0, S),)
IN_HALVES = ((0, HALF), (HALF, HALF))
FIRST_PIECES = ((0, HALF // 2), (HALF // 2, HALF // 2), (HALF, HALF))
CHUNKS = (256, 256, 256, 128, 128)
LAST = len(CHUNKS) - 1


def tile_list_wall_thinning_scores_kernel(
    tc, tab_words, tab_scales, offs, w1_words, w1_scales, w2, gain, wgs, page0, offs2, offs3, offs4, gm, w4, out
):
    nc = tc.nc
    with ExitStack() as ctx:
        keep = ctx.enter_context(tc.tile_pool(name="keep", bufs=1))
        ring = ctx.enter_context(tc.tile_pool(name="ring", bufs=2))
        psum = ctx.enter_context(tc.psum_pool(name="psum", bufs=4))

        def bank(shape):
            return psum.tile(shape, F32, name="bank")

        lists = [keep.tile([P, LIST_COLS], U16, name="list%d" % i) for i in range(4)]
        table = [keep.tile([P, T], U32, name="table%d" % a, tag="table%d" % a) for a in range(PASSES)]
        table_scales = keep.tile([P, T], U8, name="table_scales")
        v_codes = {a: keep.tile([P, S], U32, name="v_codes%d" % a, align_bytes=64) for a in range(PASSES)}
        v_scales = [keep.tile([P, S], U8, name="v_scales0", align_bytes=64)]
        w1_first = keep.tile([P, PASSES, 2 * P], U8, name="w1_first", align_bytes=64)
        w1_rest = keep.tile([P, PASSES, 2 * (H - P)], U8, name="w1_rest", align_bytes=64)
        w1_rows = w1_words.rearrange("a p c -> p a c")
        w1_planes = keep.tile([P, PASSES, H], U8, name="w1_planes", align_bytes=64)
        gain_sb = keep.tile([P, ROW_TILES], F32, name="gain_sb")
        wgs_sb = keep.tile([P, S], F32, name="wgs_sb")
        page = [keep.tile([P, T2], F32, name="page%d" % t) for t in range(ROW_TILES)]
        before = [keep.tile([P, T2], F32, name="before%d" % t) for t in range(ROW_TILES)]
        gm_sb = [keep.tile([P, ROW_TILES, w], F32, name="gm_sb%d" % c) for c, w in enumerate(CHUNKS)]
        ident = keep.tile([P, P], F32, name="ident")

        nc.gpsimd.memset(table_scales[:].bitcast(I32), 0)
        nc.vector.memset(w1_planes[:].rearrange("p a c -> p (a c)").bitcast(I32), 0)

        w2_raw = {}

        def load_table(a):
            nc.sync.dma_start(table[a][:].bitcast(I32), tab_words[a].rearrange("p t i -> p (t i)").bitcast(I32))

        def load_w2(t):
            for a in range(PASSES):
                if t == 0:
                    w2_raw[t, a] = keep.tile([P, PACK, P], F32, name="w2_first", tag="first%d" % a, align_bytes=64)
                else:
                    w2_raw[t, a] = ring.tile([P, PACK, P], F32, name="w2_raw", bufs=2 * PASSES)
                rows = w2[a * P * PACK : (a + 1) * P * PACK, t * P : (t + 1) * P]
                nc.sync.dma_start(w2_raw[t, a][:], rows.rearrange("(p i) c -> p i c", i=PACK))

        with nc.allow_non_contiguous_dma(reason="one gain value for each partition and row tile"):
            nc.gpsimd.dma_start(gain_sb[:], gain.rearrange("(t p) -> p t", p=P))
        nc.sync.dma_start(lists[0][:], offs)
        load_table(0)
        load_w2(0)
        for q in range(4):
            nc.sync.dma_start(
                table_scales[32 * q : 32 * q + 4 * PASSES, :].bitcast(I32),
                tab_scales[:, 4 * q : 4 * q + 4, :].bitcast(I32),
            )
        make_identity(nc, ident[:])
        load_table(1)
        nc.sync.dma_start(w1_first[:].bitcast(I32), w1_rows[:, :, : 2 * P].bitcast(I32))
        for q in range(4):
            nc.sync.dma_start(
                w1_planes[32 * q : 32 * q + 4, :, :].bitcast(I32),
                w1_scales[:, 4 * q : 4 * q + 4, :].rearrange("a r c -> r a c").bitcast(I32),
            )
        load_table(2)
        nc.sync.dma_start(lists[1][:], offs2)

        def gather_words(a, pieces):
            for first, width in pieces:
                nc.vector.tensor_copy(
                    v_codes[a][:, first : first + width],
                    table[a][:].indirect(lists[0][:, first // 16 : (first + width) // 16]),
                )

        w2_codes, w2_planes = {}, {}

        def quantise_w2(t):
            woven = keep.tile([P, PASSES, P, PACK], BF16, name="w2_woven%d" % t, tag="turn%d" % t, align_bytes=64)
            for a in range(PASSES):
                nc.scalar.copy(
                    woven[:, a].rearrange("p (c j) i -> p c i j", j=4),
                    w2_raw[t, a][:].rearrange("p i (c j) -> p c i j", j=4),
                )
            w2_codes[t] = keep.tile([P, PASSES * P], U32, name="w2_codes%d" % t, align_bytes=64)
            w2_planes[t] = keep.tile([P, PASSES * P], U8, name="w2_planes%d" % t, align_bytes=64)
            nc.vector.quantize_mx(
                w2_codes[t][:].bitcast(FP8X4), w2_planes[t][:], woven[:].rearrange("p a c i -> p (a c i)")
            )

        gather_words(0, WHOLE)
        nc.vector.tensor_copy(v_scales[0][:], table_scales[:].indirect(lists[0][:]))
        quantise_w2(0)
        for a in range(1, PASSES):
            v_scales.append(keep.tile([P, S], U8, name="v_scales", tag="first%d" % a, align_bytes=64))
            nc.gpsimd.memset(v_scales[a][:].bitcast(I32), 0)
            nc.sync.dma_start(
                v_scales[a][:SHIFT_ROWS, :].bitcast(I32), v_scales[0][4 * a : 4 * a + SHIFT_ROWS, :].bitcast(I32)
            )
        nc.sync.dma_start(wgs_sb[:, :HALF], wgs[:, :HALF])
        nc.sync.dma_start(page[0][:], page0[:P, :])
        load_w2(1)
        nc.sync.dma_start(w1_rest[:].bitcast(I32), w1_rows[:, :, 2 * P :].bitcast(I32))
        nc.sync.dma_start(wgs_sb[:, HALF:], wgs[:, HALF:])

        gather_words(1, WHOLE)
        gather_words(2, FIRST_PIECES)

        pieces = (FIRST_PIECES, IN_HALVES, WHOLE, WHOLE)
        units = [(t, first, width) for t in range(ROW_TILES) for first, width in pieces[t]]

        def make_h(unit):
            t, first, width = units[unit]
            w1_codes, w1_t = (w1_first, 0) if t == 0 else (w1_rest, t - 1)
            tanh_f = ring.tile([P, width], F32, name="tanh_f")
            abs_d = ring.tile([P, width], F32, name="abs_d")
            for inside in range(0, width, HALF):
                part = slice(inside, min(inside + HALF, width))
                cols = slice(first + part.start, first + part.stop)
                f_ps = bank([P, part.stop - part.start])
                d_ps = bank([P, part.stop - part.start])
                for a in range(PASSES):
                    nc.tensor.matmul_mx(
                        f_ps[:],
                        lhsT=w2_codes[t][:, a * P : (a + 1) * P].bitcast(FP8X4),
                        lhsT_scale=w2_planes[t][:, a * P : (a + 1) * P],
                        rhs=v_codes[a][:, cols].bitcast(FP8X4),
                        rhs_scale=v_scales[a][:, cols],
                        start=(a == 0),
                        stop=(a == PASSES - 1),
                    )
                    nc.tensor.matmul_mx(
                        d_ps[:],
                        lhsT=w1_codes[:, a, 2 * w1_t * P : 2 * (w1_t + 1) * P].bitcast(FP4X4),
                        lhsT_scale=w1_planes[:, a, t * P : (t + 1) * P],
                        rhs=v_codes[a][:, cols].bitcast(FP8X4),
                        rhs_scale=v_scales[a][:, cols],
                        start=(a == 0),
                        stop=(a == PASSES - 1),
                    )
                nc.scalar.activation(tanh_f[:, part], f_ps[:], ACT.Tanh)
                nc.scalar.activation(abs_d[:, part], d_ps[:], ACT.Abs)
            if 2 <= unit <= ROW_TILES:
                h_sb = keep.tile([P, width], F32, name="h_held", tag="turn%d" % (unit - 1), align_bytes=64)
            else:
                h_sb = ring.tile([P, width], F32, name="h_sb")
            nc.vector.scalar_tensor_tensor(h_sb[:], abs_d[:], gain_sb[:, t : t + 1], tanh_f[:], MULT, MULT)
            return h_sb

        def put(unit, h_sb):
            t, first, width = units[unit]
            places = lists[1][:, first // 16 : (first + width) // 16]
            nc.vector.tensor_tensor(page[t][:].indirect(places), h_sb[:], wgs_sb[:, first : first + width], MULT)

        for t in range(1, ROW_TILES):
            if t + 1 < ROW_TILES:
                load_w2(t + 1)
            nc.sync.dma_start(page[t][:], page0[t * P : (t + 1) * P, :])
        nc.sync.dma_start(lists[2][:], offs3)
        nc.sync.dma_start(lists[3][:], offs4)
        starts = [sum(CHUNKS[:c]) for c in range(len(CHUNKS))]
        gm_rows = gm.rearrange("(t p) m -> p t m", p=P)
        nc.sync.dma_start(gm_sb[0][:], gm_rows[:, :, : CHUNKS[0]])
        for t in range(ROW_TILES):
            nc.sync.dma_start(before[t][:], page0[t * P : (t + 1) * P, :])
        w4_raw = keep.tile([P, PACK, N_OUT], F32, name="w4_raw", tag="table0")
        nc.sync.dma_start(w4_raw[:], w4.rearrange("(p i) n -> p i n", i=PACK))
        for c in range(1, len(CHUNKS)):
            nc.sync.dma_start(gm_sb[c][:], gm_rows[:, :, starts[c] : starts[c] + CHUNKS[c]])

        made = make_h(0)
        for u in range(len(units)):
            if 1 <= u < ROW_TILES:
                quantise_w2(u)
            following = make_h(u + 1) if u + 1 < len(units) else None
            put(u, made)
            made = following

        w4_woven = keep.tile([P, N_OUT, PACK], BF16, name="w4_woven", align_bytes=64)
        nc.scalar.copy(
            w4_woven[:].rearrange("p (c j) i -> p c i j", j=4), w4_raw[:].rearrange("p i (c j) -> p c i j", j=4)
        )
        w4_codes = keep.tile([P, N_OUT], U32, name="w4_codes", align_bytes=64)
        w4_plane = keep.tile([P, N_OUT], U8, name="w4_plane", align_bytes=64)

        def quantise_x(c, woven):
            x_codes = ring.tile([P, CHUNKS[c]], U32, name="x_codes", align_bytes=64)
            x_plane = ring.tile([P, CHUNKS[c]], U8, name="x_plane", align_bytes=64)
            nc.vector.quantize_mx(x_codes[:].bitcast(FP8X4), x_plane[:], woven[:])
            return x_codes, x_plane

        def fetch(c):
            width = CHUNKS[c]
            cols = slice(starts[c] // 16, (starts[c] + width) // 16)
            blocks = width // P
            sums = [psum.tile([P, H], F32, name="sums") for b in range(blocks)]
            early = ROW_TILES - 1 if c == LAST else ROW_TILES
            late = bank([P, H]) if c == LAST else None
            for t in range(ROW_TILES):
                old = ring.tile([P, width], F32, name="old", bufs=6)
                nc.vector.tensor_tensor(old[:], before[t][:].indirect(lists[3][:, cols]), gm_sb[c][:, t, :], MULT)
                if c == LAST and t == ROW_TILES - 1:
                    new = keep.tile([P, width], F32, name="new_held", tag="late", align_bytes=64)
                else:
                    new = ring.tile([P, width], F32, name="new", bufs=6)
                nc.vector.tensor_tensor(new[:], page[t][:].indirect(lists[2][:, cols]), gm_sb[c][:, t, :], MULT)
                for b in range(blocks):
                    target = (sums[b] if t < early else late)[:, t * P : (t + 1) * P]
                    block = slice(b * P, (b + 1) * P)
                    nc.tensor.matmul(target, old[:, block], ident[:], start=True, stop=False, is_transpose=True)
                    nc.tensor.matmul(target, new[:, block], ident[:], start=False, stop=True, is_transpose=True)
            back = bank([P, blocks, 2, P])
            for b in range(blocks):
                x_t = ring.tile([P, H], BF16, name="x_t", bufs=3)
                for source, rows in ((sums[b], slice(0, 32 * early)), (late, slice(32 * early, P))):
                    if rows.start < rows.stop:
                        nc.scalar.copy(
                            x_t[:].rearrange("m (u p e) -> m u p e", u=2, e=2)[:, :, rows, :],
                            source[:].rearrange("m (p u e) -> m u p e", u=2, e=2)[:, :, rows, :],
                        )
                for u in range(2):
                    nc.tensor.transpose(back[:, b, u, :], x_t[:].bitcast(F32)[:, u * P : (u + 1) * P], ident[:])
            if c == LAST - 2:
                woven = keep.tile([P, width * PACK], BF16, name="x_woven_late", tag="late", align_bytes=64)
            else:
                woven = ring.tile([P, width * PACK], BF16, name="x_woven", align_bytes=64)
            nc.scalar.copy(
                woven[:].bitcast(F32).rearrange("p (b m u) -> p b m u", b=blocks, u=2),
                back[:].rearrange("p b u m -> p b m u"),
            )
            return woven

        out_rows = out.rearrange("(j p) m -> p j m", p=P)

        def score(c, x_codes, x_plane):
            width = CHUNKS[c]
            for pair in range(2):
                acc = bank([P, 2, width])
                for j in range(2):
                    n_cols = slice((2 * pair + j) * P, (2 * pair + j + 1) * P)
                    nc.tensor.matmul_mx(
                        acc[:, j, :],
                        lhsT=w4_codes[:, n_cols].bitcast(FP8X4),
                        lhsT_scale=w4_plane[:, n_cols],
                        rhs=x_codes[:].bitcast(FP8X4),
                        rhs_scale=x_plane[:],
                        start=True,
                        stop=True,
                    )
                staged = ring.tile([P, 2, width], F32, name="staged", bufs=5)
                if 2 * LAST - 2 <= 2 * c + pair <= 2 * LAST:
                    nc.vector.tensor_copy(staged[:], acc[:])
                else:
                    nc.scalar.copy(staged[:], acc[:])
                (nc.scalar if 2 * c + pair == 2 * LAST + 1 else nc.sync).dma_start(out_rows[:, 2 * pair : 2 * pair + 2, starts[c] : starts[c] + width], staged[:])

        nc.vector.quantize_mx(w4_codes[:].bitcast(FP8X4), w4_plane[:], w4_woven[:].rearrange("p n i -> p (n i)"))
        waiting = fetch(0)
        for c in range(len(CHUNKS)):
            following = fetch(c + 1) if c + 1 < len(CHUNKS) else None
            score(c, *quantise_x(c, waiting))
            waiting = following
